import numpy as np, ml_dtypes
CORES = [20,21,28,29]
N = 4
GROUPS = [[0,1],[2,3]]
def setup_inputs(rng):
    return {"x": rng.standard_normal((N, 128, 512), dtype=np.float32).astype(ml_dtypes.bfloat16)}
def reference(x):
    y = np.empty((N, 128, 512), x.dtype)
    for g in GROUPS:
        s = x[g].sum(axis=0, dtype=np.float64).astype(x[g].dtype)
        for r in g:
            y[r] = s
    return {"y": y}

@@ -1,0 +1,30 @@
+from concourse.mybir import AluOpType
+
+SCRATCH = {
+    "mine": ("sbuf", [128, 512], "bfloat16"),
+    "land": ("sbuf", [128, 512], "bfloat16"),
+}
+SEMAPHORES = ["loaded", "copied", "arrived", "sent", "stored"]
+
+
+def rank_program(g, core, T, topo):
+    rank = T.rank_of(core)
+    if rank is None:
+        return
+    group = [grp for grp in T.tables["GROUPS"] if rank in grp][0]
+    peers = [T.cores[r] for r in group if r != rank]
+    assert len(peers) == 1 and topo.chip(peers[0]) == topo.chip(core)
+    peer = peers[0]
+    rid, pid, _se = topo.addr(peer)
+
+    g.sync.dma_start(T.mine[:], T.x[:]).then_inc(T.sem.loaded, 16)
+    g.scalar.dma_start(T.y[:], T.x[:]).then_inc(T.sem.copied, 16)
+
+    g.wait_ge(T.sem.loaded, 16)
+    g.remote_dma(T.land[:], T.mine[:], T.sem.arrived, T.sem.sent, pid, rid, topo.mask(core, peer))
+
+    g.wait_ge(T.sem.arrived, 16)
+    g.wait_ge(T.sem.copied, 16)
+    g.dma_start(T.y[:], T.land[:], accum_op=AluOpType.add).then_inc(T.sem.stored, 16)
+    g.wait_ge(T.sem.stored, 16)
+    g.wait_ge(T.sem.sent, 16)

@@ -1,8 +1,8 @@
 from concourse.mybir import AluOpType
 
 SCRATCH = {
-    "mine": ("sbuf", [128, 512], "bfloat16"),
-    "land": ("sbuf", [128, 512], "bfloat16"),
+    "mine": ("dram", [128, 512], "bfloat16"),
+    "land": ("dram", [128, 512], "bfloat16"),
 }
 SEMAPHORES = ["loaded", "copied", "arrived", "sent", "stored"]
 
@@ -25,6 +25,6 @@ def rank_program(g, core, T, topo):
 
     g.wait_ge(T.sem.arrived, 16)
     g.wait_ge(T.sem.copied, 16)
-    g.dma_start(T.y[:], T.land[:], accum_op=AluOpType.add).then_inc(T.sem.stored, 16)
+    g.dma_start(T.y[:], T.land[:], accum_op=AluOpType.add, max_dma_last_dim=4096).then_inc(T.sem.stored, 16)
     g.wait_ge(T.sem.stored, 16)
     g.wait_ge(T.sem.sent, 16)

from concourse.mybir import AluOpType

SCRATCH = {
    "mine": ("dram", [128, 512], "bfloat16"),
    "land": ("dram", [128, 512], "bfloat16"),
}
SEMAPHORES = ["loaded", "copied", "arrived", "sent", "stored"]


def rank_program(g, core, T, topo):
    rank = T.rank_of(core)
    if rank is None:
        return
    group = [grp for grp in T.tables["GROUPS"] if rank in grp][0]
    peers = [T.cores[r] for r in group if r != rank]
    assert len(peers) == 1 and topo.chip(peers[0]) == topo.chip(core)
    peer = peers[0]
    rid, pid, _se = topo.addr(peer)

    g.sync.dma_start(T.mine[:], T.x[:]).then_inc(T.sem.loaded, 16)
    g.scalar.dma_start(T.y[:], T.x[:]).then_inc(T.sem.copied, 16)

    g.wait_ge(T.sem.loaded, 16)
    g.remote_dma(T.land[:], T.mine[:], T.sem.arrived, T.sem.sent, pid, rid, topo.mask(core, peer))

    g.wait_ge(T.sem.arrived, 16)
    g.wait_ge(T.sem.copied, 16)
    g.dma_start(T.y[:], T.land[:], accum_op=AluOpType.add, max_dma_last_dim=4096).then_inc(T.sem.stored, 16)
    g.wait_ge(T.sem.stored, 16)
    g.wait_ge(T.sem.sent, 16)
